import numpy as np, ml_dtypes
CORES = [211,219,227,235,243,251,83,91,99,107,115,123]
N = 12
WB, F = 5, 128
def setup_inputs(rng):
    return {"a": rng.standard_normal((N, 128, 128), dtype=np.float32).astype(ml_dtypes.bfloat16), "w": rng.standard_normal((N, 128, F), dtype=np.float32).astype(ml_dtypes.bfloat16)}
def setup_inputs_big(rng):
    d = setup_inputs(rng)
    for k in ("a", "w"): d[k] = (d[k].astype(np.float32) * 1024.0).astype(d[k].dtype)
    return d
def setup_inputs_small(rng):
    d = setup_inputs(rng)
    for k in ("a", "w"): d[k] = (d[k].astype(np.float32) * (1 / 1024.0)).astype(d[k].dtype)
    return d
def setup_inputs_apart(rng):
    d = setup_inputs(rng)
    f = (10.0 ** rng.permutation(np.linspace(-1.5, 1.5, N))).astype(np.float32).reshape(N, 1, 1)
    for k in ("a", "w"): d[k] = (d[k].astype(np.float32) * f).astype(d[k].dtype)
    return d
def reference(a, w):
    A, W = a.astype(np.float64), w.astype(np.float64)
    p = [A[j].T @ W[j] for j in range(N)]
    y = np.stack([sum(p[(r - i) % N] for i in range(WB + 1)) for r in range(N)])
    return {"y": y.astype(ml_dtypes.bfloat16 if a.dtype != np.float64 else np.float64)}

@@ -1,0 +1,90 @@
+from concourse.bass import DstId, RemoteDMATransfer
+from concourse.mybir import AluOpType
+
+BF, F32 = "bfloat16", "float32"
+SCRATCH = {
+    "a_sb": ("sbuf", [128, 128], BF),
+    "w_sb": ("sbuf", [128, 128], BF),
+    "ps": ("psum", [128, 128], F32),
+    "p_sb": ("sbuf", [128, 128], BF),
+    "l1": ("sbuf", [128, 128], BF),
+    "l4": ("sbuf", [128, 128], BF),
+    "l5": ("sbuf", [128, 128], BF),
+    "lq": ("sbuf", [128, 128], BF),
+    "y_sb": ("sbuf", [128, 128], BF),
+}
+SEMAPHORES = ["ld", "mm", "cp", "arr1", "arrf", "arrq", "sent", "va", "vd", "st"]
+
+
+def _engines(mask):
+    return bin(mask).count("1")
+
+
+def rank_program(g, core, T, topo):
+    rank = T.rank_of(core)
+    if rank is None:
+        return
+    n = len(T.cores)
+    S = T.sem
+
+    def peer(off):
+        d = T.cores[(rank + off) % n]
+        assert topo.may_write(core, d)
+        rid, pid = topo.addr(d, core)
+        return d, rid, pid, topo.mask(core, d)
+
+    g.sync.dma_start(T.a_sb[:], T.a[:]).then_inc(S.ld, 16)
+    g.scalar.dma_start(T.w_sb[:], T.w[:]).then_inc(S.ld, 16)
+
+    g.tensor.wait_ge(S.ld, 32)
+    g.tensor.matmul(T.ps[:], T.a_sb[:], T.w_sb[:], start=True, stop=True).then_inc(S.mm, 1)
+
+    g.vector.wait_ge(S.mm, 1)
+    g.vector.tensor_copy(T.p_sb[:], T.ps[:]).then_inc(S.cp, 1)
+
+    sent = 0
+    g.wait_ge(S.cp, 1)
+    _, rid, pid, m1 = peer(1)
+    g.remote_dma(out_ap=T.l1[:], in_ap=T.p_sb[:], remote_sem=S.arr1, local_sem=S.sent,
+                 pid=pid, routing_id=rid, dma_engine_mask=m1)
+    sent += _engines(m1)
+
+    _, rid4, pid4, m4 = peer(4)
+    _, rid5, pid5, m5 = peer(5)
+    mf = m4 & m5
+    g.remote_dma_fused([RemoteDMATransfer(dst_ids=[DstId(rid=rid4, pnc=pid4), DstId(rid=rid5, pnc=pid5)],
+                                          dma_engine_mask=mf, remote_sem=S.arrf,
+                                          srcs=[T.p_sb[:]], dsts=[T.l4[:], T.l5[:]], alu_op=0)],
+                       local_sem=S.sent)
+    sent += _engines(mf)
+
+    in1 = _engines(topo.mask(T.cores[(rank - 1) % n], core))
+    inf = _engines(topo.mask(T.cores[(rank - 4) % n], core) & topo.mask(T.cores[(rank - 4) % n], T.cores[(rank + 1) % n])) \
+        + _engines(topo.mask(T.cores[(rank - 5) % n], core) & topo.mask(T.cores[(rank - 5) % n], T.cores[(rank - 1) % n]))
+    inq = _engines(topo.mask(T.cores[(rank - 2) % n], core))
+
+    g.wait_ge(S.arr1, in1)
+    _, rid2, pid2, m2 = peer(2)
+    g.remote_dma_fused([RemoteDMATransfer(dst_ids=[DstId(rid=rid2, pnc=pid2)], dma_engine_mask=m2, remote_sem=S.arrq,
+                                          srcs=[T.p_sb[:], T.l1[:]], dsts=[T.lq[:]], alu_op=1)],
+                       local_sem=S.sent)
+    sent += _engines(m2)
+
+    v = g.vector
+    v.wait_ge(S.cp, 1)
+    v.wait_ge(S.arr1, in1)
+    v.tensor_tensor(T.ps[:], T.ps[:], T.l1[:], AluOpType.add).then_inc(S.va, 1)
+    v.wait_ge(S.arrf, inf)
+    v.wait_ge(S.va, 1)
+    v.tensor_tensor(T.ps[:], T.ps[:], T.l4[:], AluOpType.add).then_inc(S.va, 1)
+    v.wait_ge(S.va, 2)
+    v.tensor_tensor(T.ps[:], T.ps[:], T.l5[:], AluOpType.add).then_inc(S.va, 1)
+    v.wait_ge(S.arrq, inq)
+    v.wait_ge(S.va, 3)
+    v.tensor_tensor(T.y_sb[:], T.ps[:], T.lq[:], AluOpType.add).then_inc(S.vd, 1)
+
+    g.sync.wait_ge(S.vd, 1)
+    g.sync.dma_start(T.y[:], T.y_sb[:]).then_inc(S.st, 16)
+    g.sync.wait_ge(S.st, 16)
+
+    g.wait_ge(S.sent, sent)

@@ -3,21 +3,30 @@ from concourse.mybir import AluOpType
 
 BF, F32 = "bfloat16", "float32"
 SCRATCH = {
-    "a_sb": ("sbuf", [128, 128], BF),
-    "w_sb": ("sbuf", [128, 128], BF),
-    "ps": ("psum", [128, 128], F32),
+    "aw": ("sbuf", [128, 256], BF),
+    "ps": ("psum", [128, 512], F32),
+    "acc": ("psum", [128, 512], F32),
     "p_sb": ("sbuf", [128, 128], BF),
+    "law": ("sbuf", [128, 256], BF),
     "l1": ("sbuf", [128, 128], BF),
-    "l4": ("sbuf", [128, 128], BF),
+    "l2": ("sbuf", [128, 128], BF),
+    "l3": ("sbuf", [128, 128], BF),
     "l5": ("sbuf", [128, 128], BF),
-    "lq": ("sbuf", [128, 128], BF),
+    "ones": ("sbuf", [128, 128], BF),
+    "idn": ("sbuf", [128, 128], BF),
     "y_sb": ("sbuf", [128, 128], BF),
 }
-SEMAPHORES = ["ld", "mm", "cp", "arr1", "arrf", "arrq", "sent", "va", "vd", "st"]
+SEMAPHORES = ["ld", "mm", "cp", "one", "idm", "arr4", "arrl", "arr5", "arr2", "sent", "accd", "vd", "st"]
 
 
-def _engines(mask):
+def _count(mask):
     return bin(mask).count("1")
+
+
+def _halves(mask):
+    bits = [b for b in range(16) if (mask >> b) & 1]
+    h = len(bits) // 2
+    return sum(1 << b for b in bits[:h]), sum(1 << b for b in bits[h:])
 
 
 def rank_program(g, core, T, topo):
@@ -27,61 +36,70 @@ def rank_program(g, core, T, topo):
     n = len(T.cores)
     S = T.sem
 
-    def peer(off):
-        d = T.cores[(rank + off) % n]
-        assert topo.may_write(core, d)
-        rid, pid = topo.addr(d, core)
-        return d, rid, pid, topo.mask(core, d)
+    def masks_of(src_rank):
+        src = T.cores[src_rank % n]
+        m = -1
+        for off in range(1, 6):
+            d = T.cores[(src_rank + off) % n]
+            assert topo.may_write(src, d)
+            m &= topo.mask(src, d)
+        lo, hi = _halves(m)
+        return m, lo, hi
 
-    g.sync.dma_start(T.a_sb[:], T.a[:]).then_inc(S.ld, 16)
-    g.scalar.dma_start(T.w_sb[:], T.w[:]).then_inc(S.ld, 16)
+    def dst(off):
+        rid, pid = topo.addr(T.cores[(rank + off) % n], core)
+        return DstId(rid=rid, pnc=pid)
 
-    g.tensor.wait_ge(S.ld, 32)
-    g.tensor.matmul(T.ps[:], T.a_sb[:], T.w_sb[:], start=True, stop=True).then_inc(S.mm, 1)
+    m_all, m_lo, m_hi = masks_of(rank)
+    A, W = T.aw[:, 0:128], T.aw[:, 128:256]
+    ps, acc = T.ps[:, 0:128], T.acc[:, 0:128]
 
-    g.vector.wait_ge(S.mm, 1)
-    g.vector.tensor_copy(T.p_sb[:], T.ps[:]).then_inc(S.cp, 1)
+    g.sync.dma_start(A, T.a[:]).then_inc(S.ld, 16)
+    g.scalar.dma_start(W, T.w[:]).then_inc(S.ld, 16)
 
-    sent = 0
+    g.wait_ge(S.ld, 32)
+    d4 = dst(4)
+    g.remote_dma(out_ap=T.law[:], in_ap=T.aw[:], remote_sem=S.arr4, local_sem=S.sent,
+                 pid=d4.pnc, routing_id=d4.rid, dma_engine_mask=m_hi)
     g.wait_ge(S.cp, 1)
-    _, rid, pid, m1 = peer(1)
-    g.remote_dma(out_ap=T.l1[:], in_ap=T.p_sb[:], remote_sem=S.arr1, local_sem=S.sent,
-                 pid=pid, routing_id=rid, dma_engine_mask=m1)
-    sent += _engines(m1)
+    g.remote_dma_fused([
+        RemoteDMATransfer(dst_ids=[dst(1), dst(3)], dma_engine_mask=m_lo, remote_sem=S.arrl,
+                          srcs=[T.p_sb[:]], dsts=[T.l1[:], T.l3[:]], alu_op=0),
+        RemoteDMATransfer(dst_ids=[dst(5)], dma_engine_mask=m_hi, remote_sem=S.arr5,
+                          srcs=[T.p_sb[:]], dsts=[T.l5[:]], alu_op=0),
+    ], local_sem=S.sent)
+    d2 = dst(2)
+    g.remote_dma(out_ap=T.l2[:], in_ap=T.p_sb[:], remote_sem=S.arr2, local_sem=S.sent,
+                 pid=d2.pnc, routing_id=d2.rid, dma_engine_mask=m_all)
+    sent = _count(m_hi) + _count(m_lo) + _count(m_hi) + _count(m_all)
+    g.wait_ge(S.one, 1)
+    g.affine_select(T.idn[:], T.ones[:], [[-1, 128]], AluOpType.is_equal, 0.0, 0, 1).then_inc(S.idm, 1)
 
-    _, rid4, pid4, m4 = peer(4)
-    _, rid5, pid5, m5 = peer(5)
-    mf = m4 & m5
-    g.remote_dma_fused([RemoteDMATransfer(dst_ids=[DstId(rid=rid4, pnc=pid4), DstId(rid=rid5, pnc=pid5)],
-                                          dma_engine_mask=mf, remote_sem=S.arrf,
-                                          srcs=[T.p_sb[:]], dsts=[T.l4[:], T.l5[:]], alu_op=0)],
-                       local_sem=S.sent)
-    sent += _engines(mf)
+    in4 = _count(masks_of(rank - 4)[2])
+    inl = _count(masks_of(rank - 1)[1]) + _count(masks_of(rank - 3)[1])
+    in5 = _count(masks_of(rank - 5)[2])
+    in2 = _count(masks_of(rank - 2)[0])
 
-    in1 = _engines(topo.mask(T.cores[(rank - 1) % n], core))
-    inf = _engines(topo.mask(T.cores[(rank - 4) % n], core) & topo.mask(T.cores[(rank - 4) % n], T.cores[(rank + 1) % n])) \
-        + _engines(topo.mask(T.cores[(rank - 5) % n], core) & topo.mask(T.cores[(rank - 5) % n], T.cores[(rank - 1) % n]))
-    inq = _engines(topo.mask(T.cores[(rank - 2) % n], core))
-
-    g.wait_ge(S.arr1, in1)
-    _, rid2, pid2, m2 = peer(2)
-    g.remote_dma_fused([RemoteDMATransfer(dst_ids=[DstId(rid=rid2, pnc=pid2)], dma_engine_mask=m2, remote_sem=S.arrq,
-                                          srcs=[T.p_sb[:], T.l1[:]], dsts=[T.lq[:]], alu_op=1)],
-                       local_sem=S.sent)
-    sent += _engines(m2)
+    t = g.tensor
+    t.wait_ge(S.ld, 32)
+    t.matmul(ps, A, W, start=True, stop=True).then_inc(S.mm, 1)
+    t.matmul(acc, A, W, start=True, stop=False)
+    t.wait_ge(S.arr4, in4)
+    t.matmul(acc, T.law[:, 0:128], T.law[:, 128:256], start=False, stop=False)
+    t.wait_ge(S.idm, 1)
+    t.wait_ge(S.arrl, inl)
+    t.matmul(acc, T.idn[:], T.l1[:], start=False, stop=False)
+    t.matmul(acc, T.idn[:], T.l3[:], start=False, stop=False)
+    t.wait_ge(S.arr5, in5)
+    t.matmul(acc, T.idn[:], T.l5[:], start=False, stop=True).then_inc(S.accd, 1)
 
     v = g.vector
-    v.wait_ge(S.cp, 1)
-    v.wait_ge(S.arr1, in1)
-    v.tensor_tensor(T.ps[:], T.ps[:], T.l1[:], AluOpType.add).then_inc(S.va, 1)
-    v.wait_ge(S.arrf, inf)
-    v.wait_ge(S.va, 1)
-    v.tensor_tensor(T.ps[:], T.ps[:], T.l4[:], AluOpType.add).then_inc(S.va, 1)
-    v.wait_ge(S.va, 2)
-    v.tensor_tensor(T.ps[:], T.ps[:], T.l5[:], AluOpType.add).then_inc(S.va, 1)
-    v.wait_ge(S.arrq, inq)
-    v.wait_ge(S.va, 3)
-    v.tensor_tensor(T.y_sb[:], T.ps[:], T.lq[:], AluOpType.add).then_inc(S.vd, 1)
+    v.memset(T.ones[:], 1.0).then_inc(S.one, 1)
+    v.wait_ge(S.mm, 1)
+    v.tensor_copy(T.p_sb[:], ps).then_inc(S.cp, 1)
+    v.wait_ge(S.accd, 1)
+    v.wait_ge(S.arr2, in2)
+    v.tensor_tensor(T.y_sb[:], acc, T.l2[:], AluOpType.add).then_inc(S.vd, 1)
 
     g.sync.wait_ge(S.vd, 1)
     g.sync.dma_start(T.y[:], T.y_sb[:]).then_inc(S.st, 16)

from concourse.bass import DstId, RemoteDMATransfer
from concourse.mybir import AluOpType

BF, F32 = "bfloat16", "float32"
SCRATCH = {
    "aw": ("sbuf", [128, 256], BF),
    "ps": ("psum", [128, 512], F32),
    "acc": ("psum", [128, 512], F32),
    "p_sb": ("sbuf", [128, 128], BF),
    "law": ("sbuf", [128, 256], BF),
    "l1": ("sbuf", [128, 128], BF),
    "l2": ("sbuf", [128, 128], BF),
    "l3": ("sbuf", [128, 128], BF),
    "l5": ("sbuf", [128, 128], BF),
    "ones": ("sbuf", [128, 128], BF),
    "idn": ("sbuf", [128, 128], BF),
    "y_sb": ("sbuf", [128, 128], BF),
}
SEMAPHORES = ["ld", "mm", "cp", "one", "idm", "arr4", "arrl", "arr5", "arr2", "sent", "accd", "vd", "st"]


def _count(mask):
    return bin(mask).count("1")


def _halves(mask):
    bits = [b for b in range(16) if (mask >> b) & 1]
    h = len(bits) // 2
    return sum(1 << b for b in bits[:h]), sum(1 << b for b in bits[h:])


def rank_program(g, core, T, topo):
    rank = T.rank_of(core)
    if rank is None:
        return
    n = len(T.cores)
    S = T.sem

    def masks_of(src_rank):
        src = T.cores[src_rank % n]
        m = -1
        for off in range(1, 6):
            d = T.cores[(src_rank + off) % n]
            assert topo.may_write(src, d)
            m &= topo.mask(src, d)
        lo, hi = _halves(m)
        return m, lo, hi

    def dst(off):
        rid, pid = topo.addr(T.cores[(rank + off) % n], core)
        return DstId(rid=rid, pnc=pid)

    m_all, m_lo, m_hi = masks_of(rank)
    A, W = T.aw[:, 0:128], T.aw[:, 128:256]
    ps, acc = T.ps[:, 0:128], T.acc[:, 0:128]

    g.sync.dma_start(A, T.a[:]).then_inc(S.ld, 16)
    g.scalar.dma_start(W, T.w[:]).then_inc(S.ld, 16)

    g.wait_ge(S.ld, 32)
    d4 = dst(4)
    g.remote_dma(out_ap=T.law[:], in_ap=T.aw[:], remote_sem=S.arr4, local_sem=S.sent,
                 pid=d4.pnc, routing_id=d4.rid, dma_engine_mask=m_hi)
    g.wait_ge(S.cp, 1)
    g.remote_dma_fused([
        RemoteDMATransfer(dst_ids=[dst(1), dst(3)], dma_engine_mask=m_lo, remote_sem=S.arrl,
                          srcs=[T.p_sb[:]], dsts=[T.l1[:], T.l3[:]], alu_op=0),
        RemoteDMATransfer(dst_ids=[dst(5)], dma_engine_mask=m_hi, remote_sem=S.arr5,
                          srcs=[T.p_sb[:]], dsts=[T.l5[:]], alu_op=0),
    ], local_sem=S.sent)
    d2 = dst(2)
    g.remote_dma(out_ap=T.l2[:], in_ap=T.p_sb[:], remote_sem=S.arr2, local_sem=S.sent,
                 pid=d2.pnc, routing_id=d2.rid, dma_engine_mask=m_all)
    sent = _count(m_hi) + _count(m_lo) + _count(m_hi) + _count(m_all)
    g.wait_ge(S.one, 1)
    g.affine_select(T.idn[:], T.ones[:], [[-1, 128]], AluOpType.is_equal, 0.0, 0, 1).then_inc(S.idm, 1)

    in4 = _count(masks_of(rank - 4)[2])
    inl = _count(masks_of(rank - 1)[1]) + _count(masks_of(rank - 3)[1])
    in5 = _count(masks_of(rank - 5)[2])
    in2 = _count(masks_of(rank - 2)[0])

    t = g.tensor
    t.wait_ge(S.ld, 32)
    t.matmul(ps, A, W, start=True, stop=True).then_inc(S.mm, 1)
    t.matmul(acc, A, W, start=True, stop=False)
    t.wait_ge(S.arr4, in4)
    t.matmul(acc, T.law[:, 0:128], T.law[:, 128:256], start=False, stop=False)
    t.wait_ge(S.idm, 1)
    t.wait_ge(S.arrl, inl)
    t.matmul(acc, T.idn[:], T.l1[:], start=False, stop=False)
    t.matmul(acc, T.idn[:], T.l3[:], start=False, stop=False)
    t.wait_ge(S.arr5, in5)
    t.matmul(acc, T.idn[:], T.l5[:], start=False, stop=True).then_inc(S.accd, 1)

    v = g.vector
    v.memset(T.ones[:], 1.0).then_inc(S.one, 1)
    v.wait_ge(S.mm, 1)
    v.tensor_copy(T.p_sb[:], ps).then_inc(S.cp, 1)
    v.wait_ge(S.accd, 1)
    v.wait_ge(S.arr2, in2)
    v.tensor_tensor(T.y_sb[:], acc, T.l2[:], AluOpType.add).then_inc(S.vd, 1)

    g.sync.wait_ge(S.vd, 1)
    g.sync.dma_start(T.y[:], T.y_sb[:]).then_inc(S.st, 16)
    g.sync.wait_ge(S.st, 16)

    g.wait_ge(S.sent, sent)
